import numpy as np
import ml_dtypes


def mxq(x, axis, fmt="e4m3"):
    dtype, down = {"e4m3": (ml_dtypes.float8_e4m3fn, 7), "e5m2": (ml_dtypes.float8_e5m2, 14)}[fmt]
    v = np.moveaxis(np.asarray(x, np.float32).astype(ml_dtypes.bfloat16).astype(np.float64), axis, -1)
    blocks = v.reshape(v.shape[:-1] + (-1, 32))
    amax = np.abs(blocks).max(-1, keepdims=True)
    byte = np.maximum(np.where(amax > 0, np.frexp(amax)[1] - 1 + 127, 0) - down, 1)
    scale = np.exp2(byte - 127.0)
    codes = (blocks / scale).astype(np.float32).astype(dtype).astype(np.float64)
    return np.moveaxis((codes * scale).reshape(v.shape), -1, axis)


WIDE = False


def mx_kscale(k):
    if not WIDE:
        return np.ones(k)
    levels = np.array([10, -10, 5, -5, 0])
    if k % 512:
        return np.exp2(np.random.permutation(np.resize(levels, k // 32))).repeat(32)
    a = np.empty((k // 512, 16))
    for p in range(k // 512):
        a[p, :8] = np.random.permutation(np.resize(levels, 8))
        for g in range(8):
            far = levels[np.abs(levels - a[p, g]) >= 10]
            a[p, g + 8] = far[np.random.randint(len(far))]
    return np.exp2(a.ravel()).repeat(32)


BF16 = ml_dtypes.bfloat16


def bf(x):
    return np.asarray(x, np.float32).astype(BF16)


def f64(x):
    return np.asarray(x).astype(np.float64)


E2M1 = np.array([0.0, 0.5, 1.0, 1.5, 2.0, 3.0, 4.0, 6.0, -0.0, -0.5, -1.0, -1.5, -2.0, -3.0, -4.0, -6.0])


def pack_weight(w, fmt):
    k, n = w.shape
    w = f64(bf(w)).reshape(k // 32, 32, n)
    amax = np.abs(w).max(1)
    if fmt == "e4m3":
        byte = np.frexp(amax)[1] - 1 + 127 - 7
    else:
        mant, ex = np.frexp(amax / 6.0)
        byte = np.where(mant > 0.5, ex, ex - 1) + 127
    byte = np.clip(np.where(amax > 0, byte, 1), 1, 254)
    scaled = (w * np.exp2(127.0 - byte)[:, None, :]).reshape(k, n).astype(np.float32)
    by_word = np.ascontiguousarray(scaled.reshape(k // 512, 128, 4, n).transpose(0, 1, 3, 2))
    if fmt == "e4m3":
        words = by_word.astype(ml_dtypes.float8_e4m3fn).view(np.uint8)
    else:
        c = by_word.astype(ml_dtypes.float4_e2m1fn).view(np.uint8) & 0xF
        words = c[..., 0::2] | (c[..., 1::2] << 4)
    return np.ascontiguousarray(words), np.ascontiguousarray(byte.astype(np.uint8).reshape(k // 512, 16, n))


def unpack_weight(words, scales, fmt):
    g, p, n, _ = words.shape
    if fmt == "e4m3":
        vals = np.ascontiguousarray(words).view(ml_dtypes.float8_e4m3fn).astype(np.float64)
    else:
        nib = np.empty((g, p, n, 4), np.uint8)
        nib[..., 0::2] = words & 0xF
        nib[..., 1::2] = words >> 4
        vals = E2M1[nib]
    vals = vals * np.repeat(np.exp2(scales.astype(np.float64) - 127.0), 8, axis=1)[..., None]
    return vals.transpose(0, 1, 3, 2).reshape(g * 512, n)
def pack4(w):
    words, scales = pack_weight(w, "e2m1")
    return words.reshape(words.shape[0], 128, -1), scales


def unpack4(words, scales):
    return unpack_weight(words.reshape(words.shape[0], 128, -1, 2), scales, "e2m1")


M, K, F, A, R = 1024, 1024, 1536, 1024, 512


def draw0():
    s, t, u = mx_kscale(K), mx_kscale(F), mx_kscale(M)
    x = bf(np.random.standard_normal((M, K)) * s * u[:, None])
    w = bf(np.random.standard_normal((K, F)) / np.sqrt(K) / s[:, None] * t)
    p_words, p_scales = pack4(np.random.standard_normal((F, A)) / np.sqrt(F) / t[:, None])
    backup = bf(np.random.standard_normal((R, M)) / np.sqrt(M) / u)
    invtemp = bf((1 + 0.2 * np.random.standard_normal(M)) / u)
    vgain = bf((1 + 0.2 * np.random.standard_normal(F)) / t)
    return {"x": x, "w": w, "p_words": p_words, "p_scales": p_scales,
            "backup": backup, "invtemp": invtemp, "vgain": vgain}


def core(x, w, p_words, p_scales, backup, invtemp, vgain):
    h = np.maximum(mxq(f64(x), 1, "e4m3") @ mxq(f64(w), 0, "e4m3"), 0.0)
    logits = mxq(h, 1, "e4m3") @ unpack4(p_words, p_scales)
    policy = logits * f64(invtemp)[:, None]
    backed = mxq(f64(backup), 1, "e4m3") @ mxq(h, 0, "e4m3")
    value = backed * f64(vgain)
    return policy, value


def e4m3fn_bytes(y):
    return np.clip(np.asarray(y, np.float64), -448.0, 448.0).astype(np.float32).astype(ml_dtypes.float8_e4m3fn).view(np.uint8)


def e4m3fn_values(b):
    return np.asarray(b, np.uint8).view(ml_dtypes.float8_e4m3fn).astype(np.float64)


def setup_inputs():
    d = draw0()
    x0 = np.asarray(d['backup']).astype(np.float64)
    s = (np.max(np.abs(x0), axis=(0,), keepdims=True) / 448.0).astype(np.float32)
    out = {}
    for k, v in d.items():
        if k == 'backup':
            out['backup_bytes'] = e4m3fn_bytes(x0 / s.astype(np.float64))
            out['backup_scale'] = s
        else:
            out[k] = v
    return out


def reference(x, w, p_words, p_scales, backup_bytes, backup_scale, invtemp, vgain):
    return core(x, w, p_words, p_scales, e4m3fn_values(backup_bytes) * backup_scale.astype(np.float64), invtemp, vgain)

@@ -1,0 +1,357 @@
+from contextlib import ExitStack
+
+import concourse.mybir as mybir
+from concourse.masks import make_identity
+
+M, K, F, A, R = 1024, 1024, 1536, 1024, 512
+FLOPS = 2 * (M * K * F + M * F * A + R * M * F)
+
+F32 = mybir.dt.float32
+BF16 = mybir.dt.bfloat16
+I32 = mybir.dt.int32
+U32 = mybir.dt.uint32
+U8 = mybir.dt.uint8
+FP8 = mybir.dt.float8_e4m3fn
+FP8X4 = mybir.dt.float8_e4m3fn_x4
+FP4X4 = mybir.dt.float4_e2m1fn_x4
+ACT = mybir.ActivationFunctionType
+ALU = mybir.AluOpType
+
+P = 128
+NF = F // 512
+NS = M // 512
+
+
+def tile_policy_value_heads_s8_kernel(
+    tc, x, w, p_words, p_scales, backup_bytes, backup_scale, invtemp, vgain, policy, value
+):
+    nc = tc.nc
+    with ExitStack() as ctx:
+        keep = ctx.enter_context(tc.tile_pool(name="keep", bufs=1))
+        wstage = ctx.enter_context(tc.tile_pool(name="wstage", bufs=3))
+        xstage = ctx.enter_context(tc.tile_pool(name="xstage", bufs=4))
+        hstage = ctx.enter_context(tc.tile_pool(name="hstage", bufs=3))
+        ostage = ctx.enter_context(tc.tile_pool(name="ostage", bufs=6))
+        psum = ctx.enter_context(tc.psum_pool(name="psum", bufs=8))
+
+        def persistent(name, width, dtype):
+            return keep.tile([P, width], dtype, name=name, align_bytes=64)
+
+        def new_bank():
+            return psum.tile([P, 512], F32, name="bank")
+
+        ctx.enter_context(tc.manual_schedule())
+
+        warm = persistent("warm", 1, F32)
+        nc.vector.memset(warm[:], 0.0)
+        nc.scalar.activation(out=warm[:], in_=warm[:], func=ACT.Relu)
+        ident = persistent("ident", P, F32)
+        make_identity(nc, ident[:])
+        ps = keep.tile([P, NF, A], U8, name="ps", align_bytes=64)
+        nc.gpsimd.memset(ps[:].rearrange("p g n -> p (g n)").bitcast(I32), 0)
+        vrow = persistent("vrow", F, BF16)
+        nc.gpsimd.memset(vrow[:], 0.0)
+        ones = persistent("ones", P, BF16)
+        nc.gpsimd.memset(ones[:], 1.0)
+
+        w_raw, x_raw = {}, {}
+        x_view = x.rearrange("(s q t) k -> s t q k", s=NS, t=4)
+
+        def load_w(f, g):
+            w_raw[f, g] = keep.tile([P, 4, 512], BF16, name=f"w_raw{f}{g}", align_bytes=64)
+            nc.sync.dma_start(
+                out=w_raw[f, g][:],
+                in_=w[512 * g : 512 * (g + 1), 512 * f : 512 * (f + 1)].rearrange("(p j) c -> p j c", j=4),
+            )
+
+        def load_x(s, t):
+            x_raw[s, t] = persistent(f"x_raw{s}{t}", K, BF16)
+            nc.sync.dma_start(out=x_raw[s, t][:], in_=x_view[s, t])
+
+        load_w(0, 0)
+        load_w(0, 1)
+        for t in range(4):
+            load_x(0, t)
+        load_w(1, 0)
+        load_w(1, 1)
+        for t in range(4):
+            load_x(1, t)
+        load_w(2, 0)
+        load_w(2, 1)
+        b_raw = keep.tile([P, 4, M], U8, name="b_raw", align_bytes=64)
+        nc.sync.dma_start(out=b_raw[:], in_=backup_bytes.rearrange("(t r) k -> r t k", r=P))
+        inv16 = keep.tile([P, NS, 4], BF16, name="inv16", align_bytes=64)
+        nc.sync.dma_start(out=inv16[:], in_=invtemp.rearrange("(s q t) -> q s t", s=NS, t=4))
+        bscale = keep.tile([P, NS, 4], F32, name="bscale", align_bytes=64)
+        nc.sync.dma_start(out=bscale[:], in_=backup_scale.rearrange("o (s q t) -> q (o s) t", s=NS, t=4))
+        nc.sync.dma_start(out=vrow[0:1, :], in_=vgain.rearrange("(o c) -> o c", o=1))
+        pw = keep.tile([P, NF, 2 * A], U8, name="pw", align_bytes=64)
+        nc.sync.dma_start(out=pw[:].bitcast(I32), in_=p_words.rearrange("g p n -> p g n").bitcast(I32))
+        for c in range(4):
+            nc.sync.dma_start(
+                out=ps[32 * c : 32 * c + 4].bitcast(I32),
+                in_=p_scales[:, 4 * c : 4 * c + 4, :].rearrange("g r n -> r g n").bitcast(I32),
+            )
+
+        def copy(engine, out, in_):
+            if engine == "S":
+                nc.scalar.copy(out=out, in_=in_)
+            else:
+                nc.vector.tensor_copy(out=out, in_=in_)
+
+        w_codes, w_scales, w_grp = {}, {}, {}
+
+        def w_interleave(f, g, engine, lo=0, hi=4):
+            if (f, g) not in w_grp:
+                w_grp[f, g] = wstage.tile([P, 2048], BF16, name="w_grp", align_bytes=64)
+            out = w_grp[f, g][:].rearrange("p (t m j) -> p t m j", t=4, j=4)
+            in_ = w_raw[f, g][:].rearrange("p j (m t) -> p t m j", t=4)
+            copy(engine, out[:, lo:hi], in_[:, lo:hi])
+
+        def w_quantize(f, g):
+            w_codes[f, g] = persistent(f"w_codes{f}{g}", 512, U32)
+            w_scales[f, g] = persistent(f"w_scales{f}{g}", 512, U8)
+            nc.vector.quantize_mx(out=w_codes[f, g][:].bitcast(FP8X4), scales=w_scales[f, g][:], in_=w_grp[f, g][:])
+
+        x_codes, x_scales, x_grp = {}, {}, {}
+
+        def x_turn(s, t, engine):
+            bank = new_bank()
+            words = x_raw[s, t][:].bitcast(F32)
+            for g in range(2):
+                for u in range(2):
+                    i = 2 * g + u
+                    nc.tensor.transpose(
+                        bank[:, P * i : P * (i + 1)], words[:, 256 * g + u : 256 * (g + 1) : 2], ident[:]
+                    )
+            x_grp[s, t] = xstage.tile([P, 1024], BF16, name="x_grp", align_bytes=64)
+            copy(
+                engine,
+                x_grp[s, t][:].bitcast(F32).rearrange("p (g q u) -> p g q u", g=2, u=2),
+                bank[:].rearrange("p (g u q) -> p g q u", g=2, u=2),
+            )
+
+        def x_quantize(s, t):
+            x_codes[s, t] = persistent(f"x_codes{s}{t}", 256, U32)
+            x_scales[s, t] = persistent(f"x_scales{s}{t}", 256, U8)
+            nc.vector.quantize_mx(out=x_codes[s, t][:].bitcast(FP8X4), scales=x_scales[s, t][:], in_=x_grp[s, t][:])
+
+        h_grp, hf_codes, hf_scales, hs_codes, hs_scales, hs_grp = {}, {}, {}, {}, {}, {}
+
+        def trunk(s, f, t, engine):
+            bank = new_bank()
+            for j in range(4):
+                cols = slice(P * j, P * (j + 1))
+                for g in range(2):
+                    k_cols = slice(P * g, P * (g + 1))
+                    nc.tensor.matmul_mx(
+                        out=bank[:, cols],
+                        lhsT=w_codes[f, g][:, cols].bitcast(FP8X4),
+                        lhsT_scale=w_scales[f, g][:, cols],
+                        rhs=x_codes[s, t][:, k_cols].bitcast(FP8X4),
+                        rhs_scale=x_scales[s, t][:, k_cols],
+                        start=(g == 0),
+                        stop=(g == 1),
+                    )
+            if (s, f) not in h_grp:
+                h_grp[s, f] = persistent(f"h_grp{s}{f}", 2048, BF16)
+                hf_codes[s, f] = persistent(f"hf_codes{s}{f}", 512, U32)
+                hf_scales[s, f] = persistent(f"hf_scales{s}{f}", 512, U8)
+            out = h_grp[s, f][:, 512 * t : 512 * (t + 1)].rearrange("p (q j) -> p q j", j=4)
+            in_ = bank[:].rearrange("p (j q) -> p q j", j=4)
+            if engine == "S":
+                nc.scalar.activation(out=out, in_=in_, func=ACT.Relu)
+            else:
+                nc.vector.tensor_relu(out=out, in_=in_)
+
+        def hf_quantize(s, f):
+            for h in range(2):
+                nc.vector.quantize_mx(
+                    out=hf_codes[s, f][:, 256 * h : 256 * (h + 1)].bitcast(FP8X4),
+                    scales=hf_scales[s, f][:, 256 * h : 256 * (h + 1)],
+                    in_=h_grp[s, f][:, 1024 * h : 1024 * (h + 1)],
+                )
+
+        def h_turn(s, f, engines):
+            hs_grp[s, f] = hstage.tile([P, 2048], BF16, name="hs_grp", align_bytes=64)
+            words = h_grp[s, f][:].bitcast(F32)
+            banks = []
+            for u in range(2):
+                bank = new_bank()
+                banks.append(bank)
+                for t in range(4):
+                    nc.tensor.transpose(
+                        bank[:, P * t : P * (t + 1)], words[:, 256 * t + u : 256 * (t + 1) : 2], ident[:]
+                    )
+            for u in range(2):
+                copy(
+                    engines[u],
+                    hs_grp[s, f][:].rearrange("p (m u e t) -> p u m e t", u=2, e=2, t=4)[:, u],
+                    banks[u][:].bitcast(BF16).rearrange("p (t m e) -> p m e t", t=4, e=2),
+                )
+
+        def hs_quantize(s, f):
+            hs_codes[s, f] = persistent(f"hs_codes{s}{f}", 512, U32)
+            hs_scales[s, f] = persistent(f"hs_scales{s}{f}", 512, U8)
+            nc.vector.quantize_mx(
+                out=hs_codes[s, f][:].bitcast(FP8X4), scales=hs_scales[s, f][:], in_=hs_grp[s, f][:]
+            )
+
+        b_wide = keep.tile([P, 4, M], BF16, name="b_wide", align_bytes=64)
+        b_grp = [persistent(f"b_grp{g}", 2048, BF16) for g in range(NS)]
+        b_codes = [persistent(f"b_codes{g}", 512, U32) for g in range(NS)]
+        b_scales = [persistent(f"b_scales{g}", 512, U8) for g in range(NS)]
+
+        def b_widen(t, engine):
+            copy(engine, b_wide[:, t, :], b_raw[:, t, :].bitcast(FP8))
+
+        def b_turn(g, h):
+            bank = new_bank()
+            for a in range(2):
+                words = b_wide[:, 2 * h + a, :].bitcast(F32)
+                for u in range(2):
+                    c0 = 256 * u + P * a
+                    nc.tensor.transpose(bank[:, c0 : c0 + P], words[:, 256 * g + u : 256 * (g + 1) : 2], ident[:])
+            nc.vector.tensor_tensor(
+                out=b_grp[g][:, 1024 * h : 1024 * (h + 1)].rearrange("p (r u e) -> p r u e", u=2, e=2),
+                in0=bank[:].bitcast(BF16).rearrange("p (u r e) -> p r u e", u=2, e=2),
+                in1=bscale[:, g, :].rearrange("p (u e) -> p u e", e=2).unsqueeze(1).to_broadcast([P, 256, 2, 2]),
+                op=ALU.mult,
+            )
+
+        def b_quantize(g):
+            nc.vector.quantize_mx(out=b_codes[g][:].bitcast(FP8X4), scales=b_scales[g][:], in_=b_grp[g][:])
+
+        inv = persistent("inv", 8, F32)
+        vg = persistent("vg", F, F32)
+
+        def spread_gain():
+            for c in range(NF):
+                bank = new_bank()
+                cols = slice(512 * c, 512 * (c + 1))
+                nc.tensor.matmul(bank[:], lhsT=ones[:], rhs=vrow[:, cols], start=True, stop=True)
+                nc.scalar.copy(out=vg[:, cols], in_=bank[:])
+
+        p_view = policy.rearrange("(s q t) a -> s t q a", s=NS, t=4)
+
+        def policy_unit(s, t, n, engine):
+            bank = new_bank()
+            rows = slice(P * t, P * (t + 1))
+            for f in range(NF):
+                nc.tensor.matmul_mx(
+                    out=bank[:],
+                    lhsT=hf_codes[s, f][:, rows].bitcast(FP8X4),
+                    lhsT_scale=hf_scales[s, f][:, rows],
+                    rhs=pw[:, f, 1024 * n : 1024 * (n + 1)].bitcast(FP4X4),
+                    rhs_scale=ps[:, f, 512 * n : 512 * (n + 1)],
+                    start=(f == 0),
+                    stop=(f == NF - 1),
+                )
+            result = ostage.tile([P, 512], F32, name="p_out")
+            factor = inv[:, 4 * s + t : 4 * s + t + 1]
+            if engine == "S":
+                nc.scalar.activation(out=result[:], in_=bank[:], func=ACT.Copy, scale=factor)
+            else:
+                nc.vector.tensor_scalar(out=result[:], in0=bank[:], scalar1=factor, scalar2=None, op0=ALU.mult)
+            nc.sync.dma_start(out=p_view[s, t, :, 512 * n : 512 * (n + 1)], in_=result[:])
+
+        def value_unit(r, f):
+            bank = new_bank()
+            rows = slice(P * r, P * (r + 1))
+            cols = slice(512 * f, 512 * (f + 1))
+            for s in range(NS):
+                nc.tensor.matmul_mx(
+                    out=bank[:],
+                    lhsT=b_codes[s][:, rows].bitcast(FP8X4),
+                    lhsT_scale=b_scales[s][:, rows],
+                    rhs=hs_codes[s, f][:].bitcast(FP8X4),
+                    rhs_scale=hs_scales[s, f][:],
+                    start=(s == 0),
+                    stop=(s == NS - 1),
+                )
+            result = ostage.tile([P, 512], F32, name="v_out")
+            nc.vector.tensor_tensor(out=result[:], in0=bank[:], in1=vg[:, cols], op=ALU.mult)
+            nc.sync.dma_start(out=value[rows, cols], in_=result[:])
+
+        w_interleave(0, 0, "V")
+        w_quantize(0, 0)
+        w_interleave(0, 1, "S", 0, 2)
+        w_interleave(0, 1, "V", 2, 4)
+        w_quantize(0, 1)
+        for t in range(4):
+            x_turn(0, t, "S")
+        for t in range(4):
+            x_quantize(0, t)
+        for t in range(4):
+            trunk(0, 0, t, "S")
+        for g in range(2):
+            w_interleave(1, g, "V")
+            w_quantize(1, g)
+        for t in range(4):
+            x_turn(1, t, "S")
+        for t in range(4):
+            x_quantize(1, t)
+        for t in range(4):
+            trunk(0, 1, t, "S")
+        hf_quantize(0, 0)
+        w_interleave(2, 0, "V")
+        w_quantize(2, 0)
+        for t in range(4):
+            trunk(1, 0, t, "S")
+        w_interleave(2, 1, "V")
+        w_quantize(2, 1)
+        hf_quantize(0, 1)
+        for t in range(4):
+            b_widen(t, "V")
+        for t in range(4):
+            trunk(1, 1, t, "S")
+        hf_quantize(1, 0)
+        h_turn(0, 0, "VS")
+        for t in range(4):
+            trunk(0, 2, t, "SV"[t % 2])
+        hf_quantize(1, 1)
+        hs_quantize(0, 0)
+        h_turn(1, 0, "VS")
+        for t in range(4):
+            trunk(1, 2, t, "SV"[t % 2])
+        hf_quantize(0, 2)
+        hs_quantize(1, 0)
+        nc.scalar.copy(out=inv[:], in_=inv16[:].rearrange("p s t -> p (s t)"))
+        policy_unit(0, 0, 0, "S")
+        policy_unit(0, 0, 1, "S")
+        b_turn(0, 0)
+        b_turn(0, 1)
+        policy_unit(0, 1, 0, "S")
+        policy_unit(0, 1, 1, "S")
+        hf_quantize(1, 2)
+        b_turn(1, 0)
+        b_turn(1, 1)
+        b_quantize(0)
+        spread_gain()
+        policy_unit(0, 2, 0, "S")
+        policy_unit(0, 2, 1, "S")
+        h_turn(0, 1, "VS")
+        b_quantize(1)
+        policy_unit(0, 3, 0, "S")
+        policy_unit(0, 3, 1, "V")
+        h_turn(1, 1, "VS")
+        hs_quantize(0, 1)
+        for r in range(4):
+            value_unit(r, 0)
+        h_turn(0, 2, "VS")
+        hs_quantize(1, 1)
+        policy_unit(1, 0, 0, "S")
+        policy_unit(1, 0, 1, "S")
+        h_turn(1, 2, "VS")
+        hs_quantize(0, 2)
+        for r in range(4):
+            value_unit(r, 1)
+        hs_quantize(1, 2)
+        policy_unit(1, 1, 0, "S")
+        policy_unit(1, 1, 1, "S")
+        policy_unit(1, 2, 0, "S")
+        policy_unit(1, 2, 1, "S")
+        for r in range(4):
+            value_unit(r, 2)
+        policy_unit(1, 3, 0, "S")
+        policy_unit(1, 3, 1, "V")

@@ -31,7 +31,7 @@ def tile_policy_value_heads_s8_kernel(
         wstage = ctx.enter_context(tc.tile_pool(name="wstage", bufs=3))
         xstage = ctx.enter_context(tc.tile_pool(name="xstage", bufs=4))
         hstage = ctx.enter_context(tc.tile_pool(name="hstage", bufs=3))
-        ostage = ctx.enter_context(tc.tile_pool(name="ostage", bufs=6))
+        ostage = ctx.enter_context(tc.tile_pool(name="ostage", bufs=4))
         psum = ctx.enter_context(tc.psum_pool(name="psum", bufs=8))
 
         def persistent(name, width, dtype):
@@ -50,9 +50,9 @@ def tile_policy_value_heads_s8_kernel(
         ps = keep.tile([P, NF, A], U8, name="ps", align_bytes=64)
         nc.gpsimd.memset(ps[:].rearrange("p g n -> p (g n)").bitcast(I32), 0)
         vrow = persistent("vrow", F, BF16)
-        nc.gpsimd.memset(vrow[:], 0.0)
+        nc.vector.memset(vrow[:], 0.0)
         ones = persistent("ones", P, BF16)
-        nc.gpsimd.memset(ones[:], 1.0)
+        nc.vector.memset(ones[:], 1.0)
 
         w_raw, x_raw = {}, {}
         x_view = x.rearrange("(s q t) k -> s t q k", s=NS, t=4)
@@ -72,6 +72,7 @@ def tile_policy_value_heads_s8_kernel(
         load_w(0, 1)
         for t in range(4):
             load_x(0, t)
+        nc.sync.dma_start(out=vrow[0:1, :], in_=vgain.rearrange("(o c) -> o c", o=1))
         load_w(1, 0)
         load_w(1, 1)
         for t in range(4):
@@ -84,7 +85,6 @@ def tile_policy_value_heads_s8_kernel(
         nc.sync.dma_start(out=inv16[:], in_=invtemp.rearrange("(s q t) -> q s t", s=NS, t=4))
         bscale = keep.tile([P, NS, 4], F32, name="bscale", align_bytes=64)
         nc.sync.dma_start(out=bscale[:], in_=backup_scale.rearrange("o (s q t) -> q (o s) t", s=NS, t=4))
-        nc.sync.dma_start(out=vrow[0:1, :], in_=vgain.rearrange("(o c) -> o c", o=1))
         pw = keep.tile([P, NF, 2 * A], U8, name="pw", align_bytes=64)
         nc.sync.dma_start(out=pw[:].bitcast(I32), in_=p_words.rearrange("g p n -> p g n").bitcast(I32))
         for c in range(4):
@@ -172,23 +172,37 @@ def tile_policy_value_heads_s8_kernel(
                     in_=h_grp[s, f][:, 1024 * h : 1024 * (h + 1)],
                 )
 
-        def h_turn(s, f, engines):
-            hs_grp[s, f] = hstage.tile([P, 2048], BF16, name="hs_grp", align_bytes=64)
-            words = h_grp[s, f][:].bitcast(F32)
-            banks = []
-            for u in range(2):
-                bank = new_bank()
-                banks.append(bank)
-                for t in range(4):
-                    nc.tensor.transpose(
-                        bank[:, P * t : P * (t + 1)], words[:, 256 * t + u : 256 * (t + 1) : 2], ident[:]
+        h_flat = {}
+
+        def h_flatten(s, f, engine):
+            h_flat[s, f] = hstage.tile([P, 1024], F32, name="h_flat")
+            copy(
+                engine,
+                h_flat[s, f][:].rearrange("p (i u q) -> p i u q", i=4, u=2),
+                h_grp[s, f][:].bitcast(F32).rearrange("p (i q u) -> p i u q", i=4, u=2),
+            )
+
+        def h_turn(f, engines, ss=(0, 1)):
+            banks = {}
+            for s in ss:
+                hs_grp[s, f] = hstage.tile([P, 2048], BF16, name="hs_grp", align_bytes=64)
+                words = h_grp[s, f][:].bitcast(F32)
+                for u in range(2):
+                    banks[s, u] = new_bank()
+                    for t in range(4):
+                        if (s, f) in h_flat:
+                            c0 = 256 * t + P * u
+                            in_ = h_flat[s, f][:, c0 : c0 + P]
+                        else:
+                            in_ = words[:, 256 * t + u : 256 * (t + 1) : 2]
+                        nc.tensor.transpose(banks[s, u][:, P * t : P * (t + 1)], in_, ident[:])
+            for s in ss:
+                for u in range(2):
+                    copy(
+                        engines[2 * s + u],
+                        hs_grp[s, f][:].rearrange("p (m u e t) -> p u m e t", u=2, e=2, t=4)[:, u],
+                        banks[s, u][:].bitcast(BF16).rearrange("p (t m e) -> p m e t", t=4, e=2),
                     )
-            for u in range(2):
-                copy(
-                    engines[u],
-                    hs_grp[s, f][:].rearrange("p (m u e t) -> p u m e t", u=2, e=2, t=4)[:, u],
-                    banks[u][:].bitcast(BF16).rearrange("p (t m e) -> p m e t", t=4, e=2),
-                )
 
         def hs_quantize(s, f):
             hs_codes[s, f] = persistent(f"hs_codes{s}{f}", 512, U32)
@@ -205,16 +219,35 @@ def tile_policy_value_heads_s8_kernel(
         def b_widen(t, engine):
             copy(engine, b_wide[:, t, :], b_raw[:, t, :].bitcast(FP8))
 
+        b_flat = {}
+
+        def b_flatten(t, engine):
+            b_flat[t] = persistent(f"b_flat{t}", 512, F32)
+            copy(
+                engine,
+                b_flat[t][:].rearrange("p (g u q) -> p g u q", g=2, u=2),
+                b_wide[:, t, :].bitcast(F32).rearrange("p (g q u) -> p g u q", g=2, u=2),
+            )
+
+        b_bank = {}
+
         def b_turn(g, h):
             bank = new_bank()
+            b_bank[g, h] = bank
             for a in range(2):
                 words = b_wide[:, 2 * h + a, :].bitcast(F32)
                 for u in range(2):
                     c0 = 256 * u + P * a
-                    nc.tensor.transpose(bank[:, c0 : c0 + P], words[:, 256 * g + u : 256 * (g + 1) : 2], ident[:])
+                    if 2 * h + a in b_flat:
+                        in_ = b_flat[2 * h + a][:, 256 * g + P * u : 256 * g + P * (u + 1)]
+                    else:
+                        in_ = words[:, 256 * g + u : 256 * (g + 1) : 2]
+                    nc.tensor.transpose(bank[:, c0 : c0 + P], in_, ident[:])
+
+        def b_scale(g, h):
             nc.vector.tensor_tensor(
                 out=b_grp[g][:, 1024 * h : 1024 * (h + 1)].rearrange("p (r u e) -> p r u e", u=2, e=2),
-                in0=bank[:].bitcast(BF16).rearrange("p (u r e) -> p r u e", u=2, e=2),
+                in0=b_bank[g, h][:].bitcast(BF16).rearrange("p (u r e) -> p r u e", u=2, e=2),
                 in1=bscale[:, g, :].rearrange("p (u e) -> p u e", e=2).unsqueeze(1).to_broadcast([P, 256, 2, 2]),
                 op=ALU.mult,
             )
@@ -231,6 +264,9 @@ def tile_policy_value_heads_s8_kernel(
                 cols = slice(512 * c, 512 * (c + 1))
                 nc.tensor.matmul(bank[:], lhsT=ones[:], rhs=vrow[:, cols], start=True, stop=True)
                 nc.scalar.copy(out=vg[:, cols], in_=bank[:])
+
+        def load_inv():
+            nc.scalar.copy(out=inv[:], in_=inv16[:].rearrange("p s t -> p (s t)"))
 
         p_view = policy.rearrange("(s q t) a -> s t q a", s=NS, t=4)
 
@@ -273,19 +309,20 @@ def tile_policy_value_heads_s8_kernel(
             nc.vector.tensor_tensor(out=result[:], in0=bank[:], in1=vg[:, cols], op=ALU.mult)
             nc.sync.dma_start(out=value[rows, cols], in_=result[:])
 
-        w_interleave(0, 0, "V")
-        w_quantize(0, 0)
-        w_interleave(0, 1, "S", 0, 2)
-        w_interleave(0, 1, "V", 2, 4)
-        w_quantize(0, 1)
+        for g in range(2):
+            w_interleave(0, g, "V")
+        for g in range(2):
+            w_quantize(0, g)
         for t in range(4):
             x_turn(0, t, "S")
+        spread_gain()
         for t in range(4):
             x_quantize(0, t)
         for t in range(4):
             trunk(0, 0, t, "S")
         for g in range(2):
             w_interleave(1, g, "V")
+        for g in range(2):
             w_quantize(1, g)
         for t in range(4):
             x_turn(1, t, "S")
@@ -293,65 +330,68 @@ def tile_policy_value_heads_s8_kernel(
             x_quantize(1, t)
         for t in range(4):
             trunk(0, 1, t, "S")
-        hf_quantize(0, 0)
-        w_interleave(2, 0, "V")
-        w_quantize(2, 0)
+        for g in range(2):
+            w_interleave(2, g, "V")
+        for g in range(2):
+            w_quantize(2, g)
         for t in range(4):
             trunk(1, 0, t, "S")
-        w_interleave(2, 1, "V")
-        w_quantize(2, 1)
-        hf_quantize(0, 1)
+        hf_quantize(0, 0)
         for t in range(4):
             b_widen(t, "V")
         for t in range(4):
             trunk(1, 1, t, "S")
+        hf_quantize(0, 1)
         hf_quantize(1, 0)
-        h_turn(0, 0, "VS")
         for t in range(4):
-            trunk(0, 2, t, "SV"[t % 2])
+            trunk(0, 2, t, "S")
+        for t in range(4):
+            b_flatten(t, "V")
+        h_flatten(0, 0, "V")
+        h_flatten(1, 0, "V")
         hf_quantize(1, 1)
-        hs_quantize(0, 0)
-        h_turn(1, 0, "VS")
         for t in range(4):
-            trunk(1, 2, t, "SV"[t % 2])
+            trunk(1, 2, t, "SSVS"[t])
         hf_quantize(0, 2)
-        hs_quantize(1, 0)
-        nc.scalar.copy(out=inv[:], in_=inv16[:].rearrange("p s t -> p (s t)"))
-        policy_unit(0, 0, 0, "S")
-        policy_unit(0, 0, 1, "S")
-        b_turn(0, 0)
-        b_turn(0, 1)
-        policy_unit(0, 1, 0, "S")
-        policy_unit(0, 1, 1, "S")
+        load_inv()
+        for n in range(2):
+            policy_unit(0, 0, n, "S")
+        h_turn(0, "VSVS")
         hf_quantize(1, 2)
-        b_turn(1, 0)
-        b_turn(1, 1)
+        for g in range(2):
+            for h in range(2):
+                b_turn(g, h)
+        h_flatten(0, 1, "S")
+        for g in range(2):
+            for h in range(2):
+                b_scale(g, h)
+        for t in range(1, 4):
+            for n in range(2):
+                policy_unit(0, t, n, "S")
+        h_flatten(1, 1, "S")
+        hs_quantize(0, 0)
+        hs_quantize(1, 0)
         b_quantize(0)
-        spread_gain()
-        policy_unit(0, 2, 0, "S")
-        policy_unit(0, 2, 1, "S")
-        h_turn(0, 1, "VS")
         b_quantize(1)
-        policy_unit(0, 3, 0, "S")
-        policy_unit(0, 3, 1, "V")
-        h_turn(1, 1, "VS")
-        hs_quantize(0, 1)
+        for n in range(2):
+            policy_unit(1, 0, n, "S")
+        h_turn(1, "SVSS")
+        h_flatten(0, 2, "S")
+        h_flatten(1, 2, "S")
         for r in range(4):
             value_unit(r, 0)
-        h_turn(0, 2, "VS")
+        for n in range(2):
+            policy_unit(1, 1, n, "S")
+        hs_quantize(0, 1)
         hs_quantize(1, 1)
-        policy_unit(1, 0, 0, "S")
-        policy_unit(1, 0, 1, "S")
-        h_turn(1, 2, "VS")
-        hs_quantize(0, 2)
+        h_turn(2, "SVSS")
         for r in range(4):
             value_unit(r, 1)
+        hs_quantize(0, 2)
         hs_quantize(1, 2)
-        policy_unit(1, 1, 0, "S")
-        policy_unit(1, 1, 1, "S")
-        policy_unit(1, 2, 0, "S")
-        policy_unit(1, 2, 1, "S")
+        for n in range(2):
+            policy_unit(1, 2, n, "S")
         for r in range(4):
             value_unit(r, 2)
-        policy_unit(1, 3, 0, "S")
-        policy_unit(1, 3, 1, "V")
+        for n in range(2):
+            policy_unit(1, 3, n, "SV"[n])

from contextlib import ExitStack

import concourse.mybir as mybir
from concourse.masks import make_identity

M, K, F, A, R = 1024, 1024, 1536, 1024, 512
FLOPS = 2 * (M * K * F + M * F * A + R * M * F)

F32 = mybir.dt.float32
BF16 = mybir.dt.bfloat16
I32 = mybir.dt.int32
U32 = mybir.dt.uint32
U8 = mybir.dt.uint8
FP8 = mybir.dt.float8_e4m3fn
FP8X4 = mybir.dt.float8_e4m3fn_x4
FP4X4 = mybir.dt.float4_e2m1fn_x4
ACT = mybir.ActivationFunctionType
ALU = mybir.AluOpType

P = 128
NF = F // 512
NS = M // 512


def tile_policy_value_heads_s8_kernel(
    tc, x, w, p_words, p_scales, backup_bytes, backup_scale, invtemp, vgain, policy, value
):
    nc = tc.nc
    with ExitStack() as ctx:
        keep = ctx.enter_context(tc.tile_pool(name="keep", bufs=1))
        wstage = ctx.enter_context(tc.tile_pool(name="wstage", bufs=3))
        xstage = ctx.enter_context(tc.tile_pool(name="xstage", bufs=4))
        hstage = ctx.enter_context(tc.tile_pool(name="hstage", bufs=3))
        ostage = ctx.enter_context(tc.tile_pool(name="ostage", bufs=4))
        psum = ctx.enter_context(tc.psum_pool(name="psum", bufs=8))

        def persistent(name, width, dtype):
            return keep.tile([P, width], dtype, name=name, align_bytes=64)

        def new_bank():
            return psum.tile([P, 512], F32, name="bank")

        ctx.enter_context(tc.manual_schedule())

        warm = persistent("warm", 1, F32)
        nc.vector.memset(warm[:], 0.0)
        nc.scalar.activation(out=warm[:], in_=warm[:], func=ACT.Relu)
        ident = persistent("ident", P, F32)
        make_identity(nc, ident[:])
        ps = keep.tile([P, NF, A], U8, name="ps", align_bytes=64)
        nc.gpsimd.memset(ps[:].rearrange("p g n -> p (g n)").bitcast(I32), 0)
        vrow = persistent("vrow", F, BF16)
        nc.vector.memset(vrow[:], 0.0)
        ones = persistent("ones", P, BF16)
        nc.vector.memset(ones[:], 1.0)

        w_raw, x_raw = {}, {}
        x_view = x.rearrange("(s q t) k -> s t q k", s=NS, t=4)

        def load_w(f, g):
            w_raw[f, g] = keep.tile([P, 4, 512], BF16, name=f"w_raw{f}{g}", align_bytes=64)
            nc.sync.dma_start(
                out=w_raw[f, g][:],
                in_=w[512 * g : 512 * (g + 1), 512 * f : 512 * (f + 1)].rearrange("(p j) c -> p j c", j=4),
            )

        def load_x(s, t):
            x_raw[s, t] = persistent(f"x_raw{s}{t}", K, BF16)
            nc.sync.dma_start(out=x_raw[s, t][:], in_=x_view[s, t])

        load_w(0, 0)
        load_w(0, 1)
        for t in range(4):
            load_x(0, t)
        nc.sync.dma_start(out=vrow[0:1, :], in_=vgain.rearrange("(o c) -> o c", o=1))
        load_w(1, 0)
        load_w(1, 1)
        for t in range(4):
            load_x(1, t)
        load_w(2, 0)
        load_w(2, 1)
        b_raw = keep.tile([P, 4, M], U8, name="b_raw", align_bytes=64)
        nc.sync.dma_start(out=b_raw[:], in_=backup_bytes.rearrange("(t r) k -> r t k", r=P))
        inv16 = keep.tile([P, NS, 4], BF16, name="inv16", align_bytes=64)
        nc.sync.dma_start(out=inv16[:], in_=invtemp.rearrange("(s q t) -> q s t", s=NS, t=4))
        bscale = keep.tile([P, NS, 4], F32, name="bscale", align_bytes=64)
        nc.sync.dma_start(out=bscale[:], in_=backup_scale.rearrange("o (s q t) -> q (o s) t", s=NS, t=4))
        pw = keep.tile([P, NF, 2 * A], U8, name="pw", align_bytes=64)
        nc.sync.dma_start(out=pw[:].bitcast(I32), in_=p_words.rearrange("g p n -> p g n").bitcast(I32))
        for c in range(4):
            nc.sync.dma_start(
                out=ps[32 * c : 32 * c + 4].bitcast(I32),
                in_=p_scales[:, 4 * c : 4 * c + 4, :].rearrange("g r n -> r g n").bitcast(I32),
            )

        def copy(engine, out, in_):
            if engine == "S":
                nc.scalar.copy(out=out, in_=in_)
            else:
                nc.vector.tensor_copy(out=out, in_=in_)

        w_codes, w_scales, w_grp = {}, {}, {}

        def w_interleave(f, g, engine, lo=0, hi=4):
            if (f, g) not in w_grp:
                w_grp[f, g] = wstage.tile([P, 2048], BF16, name="w_grp", align_bytes=64)
            out = w_grp[f, g][:].rearrange("p (t m j) -> p t m j", t=4, j=4)
            in_ = w_raw[f, g][:].rearrange("p j (m t) -> p t m j", t=4)
            copy(engine, out[:, lo:hi], in_[:, lo:hi])

        def w_quantize(f, g):
            w_codes[f, g] = persistent(f"w_codes{f}{g}", 512, U32)
            w_scales[f, g] = persistent(f"w_scales{f}{g}", 512, U8)
            nc.vector.quantize_mx(out=w_codes[f, g][:].bitcast(FP8X4), scales=w_scales[f, g][:], in_=w_grp[f, g][:])

        x_codes, x_scales, x_grp = {}, {}, {}

        def x_turn(s, t, engine):
            bank = new_bank()
            words = x_raw[s, t][:].bitcast(F32)
            for g in range(2):
                for u in range(2):
                    i = 2 * g + u
                    nc.tensor.transpose(
                        bank[:, P * i : P * (i + 1)], words[:, 256 * g + u : 256 * (g + 1) : 2], ident[:]
                    )
            x_grp[s, t] = xstage.tile([P, 1024], BF16, name="x_grp", align_bytes=64)
            copy(
                engine,
                x_grp[s, t][:].bitcast(F32).rearrange("p (g q u) -> p g q u", g=2, u=2),
                bank[:].rearrange("p (g u q) -> p g q u", g=2, u=2),
            )

        def x_quantize(s, t):
            x_codes[s, t] = persistent(f"x_codes{s}{t}", 256, U32)
            x_scales[s, t] = persistent(f"x_scales{s}{t}", 256, U8)
            nc.vector.quantize_mx(out=x_codes[s, t][:].bitcast(FP8X4), scales=x_scales[s, t][:], in_=x_grp[s, t][:])

        h_grp, hf_codes, hf_scales, hs_codes, hs_scales, hs_grp = {}, {}, {}, {}, {}, {}

        def trunk(s, f, t, engine):
            bank = new_bank()
            for j in range(4):
                cols = slice(P * j, P * (j + 1))
                for g in range(2):
                    k_cols = slice(P * g, P * (g + 1))
                    nc.tensor.matmul_mx(
                        out=bank[:, cols],
                        lhsT=w_codes[f, g][:, cols].bitcast(FP8X4),
                        lhsT_scale=w_scales[f, g][:, cols],
                        rhs=x_codes[s, t][:, k_cols].bitcast(FP8X4),
                        rhs_scale=x_scales[s, t][:, k_cols],
                        start=(g == 0),
                        stop=(g == 1),
                    )
            if (s, f) not in h_grp:
                h_grp[s, f] = persistent(f"h_grp{s}{f}", 2048, BF16)
                hf_codes[s, f] = persistent(f"hf_codes{s}{f}", 512, U32)
                hf_scales[s, f] = persistent(f"hf_scales{s}{f}", 512, U8)
            out = h_grp[s, f][:, 512 * t : 512 * (t + 1)].rearrange("p (q j) -> p q j", j=4)
            in_ = bank[:].rearrange("p (j q) -> p q j", j=4)
            if engine == "S":
                nc.scalar.activation(out=out, in_=in_, func=ACT.Relu)
            else:
                nc.vector.tensor_relu(out=out, in_=in_)

        def hf_quantize(s, f):
            for h in range(2):
                nc.vector.quantize_mx(
                    out=hf_codes[s, f][:, 256 * h : 256 * (h + 1)].bitcast(FP8X4),
                    scales=hf_scales[s, f][:, 256 * h : 256 * (h + 1)],
                    in_=h_grp[s, f][:, 1024 * h : 1024 * (h + 1)],
                )

        h_flat = {}

        def h_flatten(s, f, engine):
            h_flat[s, f] = hstage.tile([P, 1024], F32, name="h_flat")
            copy(
                engine,
                h_flat[s, f][:].rearrange("p (i u q) -> p i u q", i=4, u=2),
                h_grp[s, f][:].bitcast(F32).rearrange("p (i q u) -> p i u q", i=4, u=2),
            )

        def h_turn(f, engines, ss=(0, 1)):
            banks = {}
            for s in ss:
                hs_grp[s, f] = hstage.tile([P, 2048], BF16, name="hs_grp", align_bytes=64)
                words = h_grp[s, f][:].bitcast(F32)
                for u in range(2):
                    banks[s, u] = new_bank()
                    for t in range(4):
                        if (s, f) in h_flat:
                            c0 = 256 * t + P * u
                            in_ = h_flat[s, f][:, c0 : c0 + P]
                        else:
                            in_ = words[:, 256 * t + u : 256 * (t + 1) : 2]
                        nc.tensor.transpose(banks[s, u][:, P * t : P * (t + 1)], in_, ident[:])
            for s in ss:
                for u in range(2):
                    copy(
                        engines[2 * s + u],
                        hs_grp[s, f][:].rearrange("p (m u e t) -> p u m e t", u=2, e=2, t=4)[:, u],
                        banks[s, u][:].bitcast(BF16).rearrange("p (t m e) -> p m e t", t=4, e=2),
                    )

        def hs_quantize(s, f):
            hs_codes[s, f] = persistent(f"hs_codes{s}{f}", 512, U32)
            hs_scales[s, f] = persistent(f"hs_scales{s}{f}", 512, U8)
            nc.vector.quantize_mx(
                out=hs_codes[s, f][:].bitcast(FP8X4), scales=hs_scales[s, f][:], in_=hs_grp[s, f][:]
            )

        b_wide = keep.tile([P, 4, M], BF16, name="b_wide", align_bytes=64)
        b_grp = [persistent(f"b_grp{g}", 2048, BF16) for g in range(NS)]
        b_codes = [persistent(f"b_codes{g}", 512, U32) for g in range(NS)]
        b_scales = [persistent(f"b_scales{g}", 512, U8) for g in range(NS)]

        def b_widen(t, engine):
            copy(engine, b_wide[:, t, :], b_raw[:, t, :].bitcast(FP8))

        b_flat = {}

        def b_flatten(t, engine):
            b_flat[t] = persistent(f"b_flat{t}", 512, F32)
            copy(
                engine,
                b_flat[t][:].rearrange("p (g u q) -> p g u q", g=2, u=2),
                b_wide[:, t, :].bitcast(F32).rearrange("p (g q u) -> p g u q", g=2, u=2),
            )

        b_bank = {}

        def b_turn(g, h):
            bank = new_bank()
            b_bank[g, h] = bank
            for a in range(2):
                words = b_wide[:, 2 * h + a, :].bitcast(F32)
                for u in range(2):
                    c0 = 256 * u + P * a
                    if 2 * h + a in b_flat:
                        in_ = b_flat[2 * h + a][:, 256 * g + P * u : 256 * g + P * (u + 1)]
                    else:
                        in_ = words[:, 256 * g + u : 256 * (g + 1) : 2]
                    nc.tensor.transpose(bank[:, c0 : c0 + P], in_, ident[:])

        def b_scale(g, h):
            nc.vector.tensor_tensor(
                out=b_grp[g][:, 1024 * h : 1024 * (h + 1)].rearrange("p (r u e) -> p r u e", u=2, e=2),
                in0=b_bank[g, h][:].bitcast(BF16).rearrange("p (u r e) -> p r u e", u=2, e=2),
                in1=bscale[:, g, :].rearrange("p (u e) -> p u e", e=2).unsqueeze(1).to_broadcast([P, 256, 2, 2]),
                op=ALU.mult,
            )

        def b_quantize(g):
            nc.vector.quantize_mx(out=b_codes[g][:].bitcast(FP8X4), scales=b_scales[g][:], in_=b_grp[g][:])

        inv = persistent("inv", 8, F32)
        vg = persistent("vg", F, F32)

        def spread_gain():
            for c in range(NF):
                bank = new_bank()
                cols = slice(512 * c, 512 * (c + 1))
                nc.tensor.matmul(bank[:], lhsT=ones[:], rhs=vrow[:, cols], start=True, stop=True)
                nc.scalar.copy(out=vg[:, cols], in_=bank[:])

        def load_inv():
            nc.scalar.copy(out=inv[:], in_=inv16[:].rearrange("p s t -> p (s t)"))

        p_view = policy.rearrange("(s q t) a -> s t q a", s=NS, t=4)

        def policy_unit(s, t, n, engine):
            bank = new_bank()
            rows = slice(P * t, P * (t + 1))
            for f in range(NF):
                nc.tensor.matmul_mx(
                    out=bank[:],
                    lhsT=hf_codes[s, f][:, rows].bitcast(FP8X4),
                    lhsT_scale=hf_scales[s, f][:, rows],
                    rhs=pw[:, f, 1024 * n : 1024 * (n + 1)].bitcast(FP4X4),
                    rhs_scale=ps[:, f, 512 * n : 512 * (n + 1)],
                    start=(f == 0),
                    stop=(f == NF - 1),
                )
            result = ostage.tile([P, 512], F32, name="p_out")
            factor = inv[:, 4 * s + t : 4 * s + t + 1]
            if engine == "S":
                nc.scalar.activation(out=result[:], in_=bank[:], func=ACT.Copy, scale=factor)
            else:
                nc.vector.tensor_scalar(out=result[:], in0=bank[:], scalar1=factor, scalar2=None, op0=ALU.mult)
            nc.sync.dma_start(out=p_view[s, t, :, 512 * n : 512 * (n + 1)], in_=result[:])

        def value_unit(r, f):
            bank = new_bank()
            rows = slice(P * r, P * (r + 1))
            cols = slice(512 * f, 512 * (f + 1))
            for s in range(NS):
                nc.tensor.matmul_mx(
                    out=bank[:],
                    lhsT=b_codes[s][:, rows].bitcast(FP8X4),
                    lhsT_scale=b_scales[s][:, rows],
                    rhs=hs_codes[s, f][:].bitcast(FP8X4),
                    rhs_scale=hs_scales[s, f][:],
                    start=(s == 0),
                    stop=(s == NS - 1),
                )
            result = ostage.tile([P, 512], F32, name="v_out")
            nc.vector.tensor_tensor(out=result[:], in0=bank[:], in1=vg[:, cols], op=ALU.mult)
            nc.sync.dma_start(out=value[rows, cols], in_=result[:])

        for g in range(2):
            w_interleave(0, g, "V")
        for g in range(2):
            w_quantize(0, g)
        for t in range(4):
            x_turn(0, t, "S")
        spread_gain()
        for t in range(4):
            x_quantize(0, t)
        for t in range(4):
            trunk(0, 0, t, "S")
        for g in range(2):
            w_interleave(1, g, "V")
        for g in range(2):
            w_quantize(1, g)
        for t in range(4):
            x_turn(1, t, "S")
        for t in range(4):
            x_quantize(1, t)
        for t in range(4):
            trunk(0, 1, t, "S")
        for g in range(2):
            w_interleave(2, g, "V")
        for g in range(2):
            w_quantize(2, g)
        for t in range(4):
            trunk(1, 0, t, "S")
        hf_quantize(0, 0)
        for t in range(4):
            b_widen(t, "V")
        for t in range(4):
            trunk(1, 1, t, "S")
        hf_quantize(0, 1)
        hf_quantize(1, 0)
        for t in range(4):
            trunk(0, 2, t, "S")
        for t in range(4):
            b_flatten(t, "V")
        h_flatten(0, 0, "V")
        h_flatten(1, 0, "V")
        hf_quantize(1, 1)
        for t in range(4):
            trunk(1, 2, t, "SSVS"[t])
        hf_quantize(0, 2)
        load_inv()
        for n in range(2):
            policy_unit(0, 0, n, "S")
        h_turn(0, "VSVS")
        hf_quantize(1, 2)
        for g in range(2):
            for h in range(2):
                b_turn(g, h)
        h_flatten(0, 1, "S")
        for g in range(2):
            for h in range(2):
                b_scale(g, h)
        for t in range(1, 4):
            for n in range(2):
                policy_unit(0, t, n, "S")
        h_flatten(1, 1, "S")
        hs_quantize(0, 0)
        hs_quantize(1, 0)
        b_quantize(0)
        b_quantize(1)
        for n in range(2):
            policy_unit(1, 0, n, "S")
        h_turn(1, "SVSS")
        h_flatten(0, 2, "S")
        h_flatten(1, 2, "S")
        for r in range(4):
            value_unit(r, 0)
        for n in range(2):
            policy_unit(1, 1, n, "S")
        hs_quantize(0, 1)
        hs_quantize(1, 1)
        h_turn(2, "SVSS")
        for r in range(4):
            value_unit(r, 1)
        hs_quantize(0, 2)
        hs_quantize(1, 2)
        for n in range(2):
            policy_unit(1, 2, n, "S")
        for r in range(4):
            value_unit(r, 2)
        for n in range(2):
            policy_unit(1, 3, n, "SV"[n])
